import numpy as np
import ml_dtypes


def mxq(x, axis, fmt="e4m3"):
    dtype, down = {"e4m3": (ml_dtypes.float8_e4m3fn, 7), "e5m2": (ml_dtypes.float8_e5m2, 14)}[fmt]
    v = np.moveaxis(np.asarray(x, np.float32).astype(ml_dtypes.bfloat16).astype(np.float64), axis, -1)
    blocks = v.reshape(v.shape[:-1] + (-1, 32))
    amax = np.abs(blocks).max(-1, keepdims=True)
    byte = np.maximum(np.where(amax > 0, np.frexp(amax)[1] - 1 + 127, 0) - down, 1)
    scale = np.exp2(byte - 127.0)
    codes = (blocks / scale).astype(np.float32).astype(dtype).astype(np.float64)
    return np.moveaxis((codes * scale).reshape(v.shape), -1, axis)


WIDE = False


def mx_kscale(k):
    if not WIDE:
        return np.ones(k)
    levels = np.array([10, -10, 5, -5, 0])
    if k % 512:
        return np.exp2(np.random.permutation(np.resize(levels, k // 32))).repeat(32)
    a = np.empty((k // 512, 16))
    for p in range(k // 512):
        a[p, :8] = np.random.permutation(np.resize(levels, 8))
        for g in range(8):
            far = levels[np.abs(levels - a[p, g]) >= 10]
            a[p, g + 8] = far[np.random.randint(len(far))]
    return np.exp2(a.ravel()).repeat(32)


def f64(x):
    return np.asarray(x).astype(np.float64)


def striped(idx):
    return np.tile(np.asarray(idx).reshape(-1, 16).T, (8, 1)).astype(np.uint16)


def unstriped(offs):
    return offs[:16].T.reshape(-1).astype(np.int64)


E2M1 = np.array([0.0, 0.5, 1.0, 1.5, 2.0, 3.0, 4.0, 6.0, -0.0, -0.5, -1.0, -1.5, -2.0, -3.0, -4.0, -6.0])


def pack_weight(w, fmt):
    k, n = w.shape
    w = f64(np.asarray(w, np.float32).astype(ml_dtypes.bfloat16)).reshape(k // 32, 32, n)
    amax = np.abs(w).max(1)
    if fmt == "e4m3":
        byte = np.frexp(amax)[1] - 1 + 127 - 7
    else:
        mant, ex = np.frexp(amax / 6.0)
        byte = np.where(mant > 0.5, ex, ex - 1) + 127
    byte = np.clip(np.where(amax > 0, byte, 1), 1, 254)
    scaled = (w * np.exp2(127.0 - byte)[:, None, :]).reshape(k, n).astype(np.float32)
    by_word = np.ascontiguousarray(scaled.reshape(k // 512, 128, 4, n).transpose(0, 1, 3, 2))
    if fmt == "e4m3":
        words = by_word.astype(ml_dtypes.float8_e4m3fn).view(np.uint8)
    else:
        c = by_word.astype(ml_dtypes.float4_e2m1fn).view(np.uint8) & 0xF
        words = (c[..., 0::2] | (c[..., 1::2] << 4)).reshape(k // 512, 128, 2 * n)
    return np.ascontiguousarray(words), np.ascontiguousarray(byte.astype(np.uint8).reshape(k // 512, 16, n))


def unpack_weight(words, scales, fmt):
    g, _, n = scales.shape
    words = np.ascontiguousarray(words).reshape(g, 128, n, -1)
    if fmt == "e4m3":
        vals = words.view(ml_dtypes.float8_e4m3fn).astype(np.float64)
    else:
        nib = np.empty((g, 128, n, 4), np.uint8)
        nib[..., 0::2] = words & 0xF
        nib[..., 1::2] = words >> 4
        vals = E2M1[nib]
    vals = vals * np.repeat(np.exp2(scales.astype(np.float64) - 127.0), 8, axis=1)[..., None]
    return vals.transpose(0, 1, 3, 2).reshape(g * 512, n)


def bf(x):
    return np.asarray(x, np.float32).astype(ml_dtypes.bfloat16)


def planes(Y):
    r, m = Y.shape
    b = f64(bf(Y)).reshape(r // 32, 32, m)
    amax = np.abs(b).max(1)
    byte = np.clip(np.where(amax > 0, np.frexp(amax)[1] - 1 + 127 - 7, 1), 1, 254)
    codes = (b * np.exp2(127.0 - byte)[:, None, :]).reshape(r, m).astype(np.float32).astype(ml_dtypes.float8_e4m3fn).view(np.uint8)
    words = codes.reshape(r // 512, 128, 4, m).transpose(0, 1, 3, 2)
    return np.ascontiguousarray(words), np.ascontiguousarray(byte.astype(np.uint8).reshape(r // 512, 16, m))


K, T, S, J, I, B = 1024, 1024, 2048, 512, 1024, 256


def setup_inputs():
    n = np.random.standard_normal
    idx = np.random.permutation(T)[:J]
    idx2 = np.random.permutation(S)[:I]
    fk = mx_kscale(K)
    xbp = pack_weight(n((K, S)) / fk[:, None], "e2m1")
    return {
        "xa": (n((K, T)) * 0.1 * fk[:, None]).astype(np.float32),
        "xb_words": xbp[0],
        "xb_scales": xbp[1],
        "offs": striped(idx),
        "offs2": striped(idx2),
    }


def reference(xa, xb_words, xb_scales, offs, offs2):
    idx = unstriped(offs)
    idx2 = unstriped(offs2)
    xbu = unpack_weight(xb_words, xb_scales, "e2m1")
    xaidxq = mxq(f64(xa)[:, idx], 0, "e4m3")
    xbidx2g = xbu[:, idx2]
    a = xaidxq.T @ xbidx2g
    y = a.reshape(J, B, I // B).max(axis=2) - np.mean(a, axis=1, keepdims=True)
    words, scales = planes(y)
    return y, words, scales

@@ -1,0 +1,220 @@
+from contextlib import ExitStack
+
+import concourse.mybir as mybir
+
+K, T, S, J, I, B = 1024, 1024, 2048, 512, 1024, 256
+FLOPS = 2 * K * J * I
+
+F32 = mybir.dt.float32
+BF16 = mybir.dt.bfloat16
+I32 = mybir.dt.int32
+U32 = mybir.dt.uint32
+U16 = mybir.dt.uint16
+U8 = mybir.dt.uint8
+FP8X4 = mybir.dt.float8_e4m3fn_x4
+FP4X4 = mybir.dt.float4_e2m1fn_x4
+COPY = mybir.ActivationFunctionType.Copy
+IDENTITY = mybir.ActivationFunctionType.Identity
+ADD = mybir.AluOpType.add
+MULT = mybir.AluOpType.mult
+MAX = mybir.AluOpType.max
+AXIS_X = mybir.AxisListType.X
+
+P = 128
+PACK = 4
+PASSES = K // (P * PACK)
+BANK = 512
+HALVES = I // BANK
+GROUP = I // B
+LIST_ROWS = 16
+
+
+def tile_list_best_of_column_groups_pl_kernel(tc, xa, xb_words, xb_scales, offs, offs2, out_0, out_1, out_2):
+    nc = tc.nc
+    with ExitStack() as ctx:
+        sb = ctx.enter_context(tc.tile_pool(name="sb", bufs=1))
+        psum = ctx.enter_context(tc.psum_pool(name="psum", bufs=1))
+
+        def tile(shape, dtype, name):
+            return sb.tile(shape, dtype, name=name, align_bytes=64)
+
+        list_a = tile([P, J // LIST_ROWS], U16, "list_a")
+        list_b = tile([P, I // LIST_ROWS], U16, "list_b")
+        word_table = [tile([P, S], U16, f"word_table{z}") for z in range(PASSES)]
+        scale_table = tile([P, S], U8, "scale_table")
+        raw = [[tile([P, 2, T // 2], F32, f"raw{g}_{c}") for c in range(2)] for g in range(2 * PASSES)]
+        pair_table = [tile([P, T, 2], BF16, f"pair_table{g}") for g in range(2 * PASSES)]
+        picked = [tile([P, 2, J], U32, f"picked{z}") for z in range(PASSES)]
+        woven = [[tile([P, J * 2], BF16, f"woven{z}_{c}") for c in range(2)] for z in range(PASSES)]
+        a_codes = [tile([P, J], U32, f"a_codes{z}") for z in range(PASSES)]
+        a_scales = [tile([P, J], U8, f"a_scales{z}") for z in range(PASSES)]
+        b_words = [[tile([P, BANK], U16, f"b_words{z}_{h}") for h in range(HALVES)] for z in range(PASSES)]
+        picked_scales = tile([P, I], U8, "picked_scales")
+        b_scales = tile([P, PASSES, I], U8, "b_scales")
+        acc = [[psum.tile([P, BANK], F32, name=f"acc{t}_{h}") for h in range(HALVES)] for t in range(PACK)]
+        best = [tile([P, B], F32, f"best{t}") for t in range(PACK)]
+        carry = [tile([P, 1], F32, f"carry{t}") for t in range(PACK)]
+        neg_mean = [tile([P, 1], F32, f"neg_mean{t}") for t in range(PACK)]
+        scaled = tile([P, BANK], BF16, "scaled")
+        y = tile([P, PACK, B], F32, "y")
+        y_woven = tile([P, B * PACK], BF16, "y_woven")
+        y_codes = tile([P, B], U32, "y_codes")
+        y_scales = tile([P, B], U8, "y_scales")
+
+        def load_words(z):
+            nc.sync.dma_start(out=word_table[z][:].bitcast(I32), in_=xb_words[z].bitcast(I32))
+
+        def load_raw(g, c):
+            z, u = divmod(g, 2)
+            rows = xa[z * P * PACK : (z + 1) * P * PACK, :].rearrange("(p t) w -> p t w", t=PACK)
+            nc.sync.dma_start(out=raw[g][c][:], in_=rows[:, 2 * u : 2 * u + 2, c * (T // 2) : (c + 1) * (T // 2)])
+
+        def round_pairs(g):
+            for c in range(2):
+                nc.scalar.activation(
+                    out=pair_table[g][:, c * (T // 2) : (c + 1) * (T // 2), :],
+                    in_=raw[g][c][:].rearrange("p e w -> p w e"),
+                    func=COPY,
+                )
+
+        def pick_pairs(g):
+            z, u = divmod(g, 2)
+            window = pair_table[g][:].rearrange("p w e -> p (w e)").bitcast(U32)
+            nc.vector.tensor_copy(out=picked[z][:, u, :], in_=window.indirect(list_a[:]))
+
+        def pick_words(z, h):
+            cols = BANK // LIST_ROWS
+            nc.vector.tensor_copy(
+                out=b_words[z][h][:], in_=word_table[z][:].indirect(list_b[:, h * cols : (h + 1) * cols])
+            )
+
+        def weave(z, c, copy, words):
+            tiles = slice(2 * c, 2 * c + 2)
+            copy(
+                out=woven[z][c][:].bitcast(words).rearrange("p (t m n u) -> p m t n u", t=2, n=2, u=2),
+                in_=picked[z][:].bitcast(words).rearrange("p u (m n t) -> p m t n u", n=2, t=PACK)[:, :, tiles],
+            )
+
+        def quantize_a(z, c):
+            cols = slice(c * J // 2, (c + 1) * J // 2)
+            nc.vector.quantize_mx(
+                out=a_codes[z][:, cols].bitcast(FP8X4), scales=a_scales[z][:, cols], in_=woven[z][c][:]
+            )
+
+        def multiply(z, t, h):
+            rows = slice(t * P, (t + 1) * P)
+            nc.tensor.matmul_mx(
+                out=acc[t][h][:],
+                lhsT=a_codes[z][:, rows].bitcast(FP8X4),
+                lhsT_scale=a_scales[z][:, rows],
+                rhs=b_words[z][h][:].bitcast(FP4X4),
+                rhs_scale=b_scales[:, z, h * BANK : (h + 1) * BANK],
+                start=(z == 0),
+                stop=(z == PASSES - 1),
+            )
+
+        def best_of_bank(t, h):
+            groups = BANK // GROUP
+            nc.vector.tensor_reduce(
+                out=best[t][:, h * groups : (h + 1) * groups],
+                in_=acc[t][h][:].rearrange("p (b g) -> p b g", g=GROUP),
+                axis=AXIS_X,
+                op=MAX,
+            )
+
+        def sum_of_bank(t, h):
+            if h == 0:
+                nc.scalar.activation(
+                    out=scaled[:], in_=acc[t][h][:], func=IDENTITY, scale=-1.0 / (I * BANK), accum_out=carry[t][:]
+                )
+            else:
+                nc.scalar.activation(
+                    out=scaled[:],
+                    in_=acc[t][h][:],
+                    func=IDENTITY,
+                    scale=-1.0 / I,
+                    bias=carry[t][:],
+                    accum_out=neg_mean[t][:],
+                )
+
+        def finish_rows(t, engine):
+            engine.tensor_scalar(
+                out=y[:, t, :], in0=best[t][:], scalar1=1.0, scalar2=neg_mean[t][:], op0=MULT, op1=ADD
+            )
+            nc.sync.dma_start(out=out_0.rearrange("(p t) b -> p t b", t=PACK)[:, t, :], in_=y[:, t, :])
+
+        nc.gpsimd.memset(scale_table[:].bitcast(I32)[32:64, :], 0)
+        nc.gpsimd.memset(scale_table[:].bitcast(I32)[64:P, :], 0)
+        nc.gpsimd.memset(b_scales[:].rearrange("p z c -> p (z c)").bitcast(I32), 0)
+
+        nc.sync.dma_start(list_b[:], offs2)
+        nc.sync.dma_start(
+            out=scale_table[:].bitcast(I32)[0:32, :], in_=xb_scales.bitcast(I32).rearrange("z q c -> q z c")
+        )
+        load_raw(0, 0)
+        load_words(0)
+        nc.sync.dma_start(list_a[:], offs)
+        load_raw(0, 1)
+        load_raw(1, 0)
+        load_raw(1, 1)
+        load_raw(2, 0)
+
+        nc.vector.tensor_copy(out=picked_scales[:], in_=scale_table[:].indirect(list_b[:]))
+        for q in range(P // 32):
+            nc.sync.dma_start(
+                out=b_scales[:].bitcast(I32)[32 * q : 32 * q + 4], in_=picked_scales[:].bitcast(I32)[8 * q : 8 * q + 8, :]
+            )
+        load_raw(2, 1)
+        load_words(1)
+        load_raw(3, 0)
+        load_raw(3, 1)
+        pick_words(0, 0)
+        pick_words(0, 1)
+        round_pairs(0)
+        pick_pairs(0)
+        round_pairs(1)
+        pick_pairs(1)
+        for c in range(2):
+            weave(0, c, nc.vector.tensor_copy, I32)
+        for c in range(2):
+            quantize_a(0, c)
+        for h in range(HALVES):
+            for t in range(PACK):
+                multiply(0, t, h)
+        round_pairs(2)
+        pick_words(1, 0)
+        pick_pairs(2)
+        round_pairs(3)
+        pick_words(1, 1)
+        pick_pairs(3)
+        weave(1, 0, nc.vector.tensor_copy, I32)
+        weave(1, 1, nc.scalar.copy, U32)
+        for c in range(2):
+            quantize_a(1, c)
+        for t0 in range(0, PACK, 2):
+            for h in range(HALVES):
+                multiply(1, t0, h)
+                multiply(1, t0 + 1, h)
+                sum_of_bank(t0, h)
+                best_of_bank(t0 + 1, h)
+                best_of_bank(t0, h)
+                sum_of_bank(t0 + 1, h)
+            for t in (t0, t0 + 1):
+                finish_rows(t, nc.gpsimd if t0 == 0 else nc.vector)
+
+        for c in range(2):
+            nc.vector.tensor_copy(
+                out=y_woven[:, c * 2 * B : (c + 1) * 2 * B].rearrange("p (c i t) -> p c t i", i=4, t=PACK),
+                in_=y[:, :, c * B // 2 : (c + 1) * B // 2].rearrange("p t (c i) -> p c t i", i=4),
+            )
+        for c in range(2):
+            cols = slice(c * B // 2, (c + 1) * B // 2)
+            nc.vector.quantize_mx(
+                out=y_codes[:, cols].bitcast(FP8X4), scales=y_scales[:, cols], in_=y_woven[:, c * 2 * B : (c + 1) * 2 * B]
+            )
+        nc.sync.dma_start(out=out_1[0].rearrange("p c r -> p (c r)").bitcast(I32), in_=y_codes[:].bitcast(I32))
+        for q in range(P // 32):
+            queue = nc.scalar if q % 2 else nc.sync
+            queue.dma_start(
+                out=out_2[0, 4 * q : 4 * q + 4, :].bitcast(I32), in_=y_scales[:].bitcast(I32)[32 * q : 32 * q + 4, :]
+            )

@@ -27,6 +27,7 @@ BANK = 512
 HALVES = I // BANK
 GROUP = I // B
 LIST_ROWS = 16
+LAST_SPLIT = 192
 
 
 def tile_list_best_of_column_groups_pl_kernel(tc, xa, xb_words, xb_scales, offs, offs2, out_0, out_1, out_2):
@@ -48,7 +49,7 @@ def tile_list_best_of_column_groups_pl_kernel(tc, xa, xb_words, xb_scales, offs,
         woven = [[tile([P, J * 2], BF16, f"woven{z}_{c}") for c in range(2)] for z in range(PASSES)]
         a_codes = [tile([P, J], U32, f"a_codes{z}") for z in range(PASSES)]
         a_scales = [tile([P, J], U8, f"a_scales{z}") for z in range(PASSES)]
-        b_words = [[tile([P, BANK], U16, f"b_words{z}_{h}") for h in range(HALVES)] for z in range(PASSES)]
+        b_words = {(z, h): tile([P, BANK], U16, f"b_words{z}_{h}") for z, h in ((0, 0), (0, 1), (1, 0))}
         picked_scales = tile([P, I], U8, "picked_scales")
         b_scales = tile([P, PASSES, I], U8, "b_scales")
         acc = [[psum.tile([P, BANK], F32, name=f"acc{t}_{h}") for h in range(HALVES)] for t in range(PACK)]
@@ -57,7 +58,8 @@ def tile_list_best_of_column_groups_pl_kernel(tc, xa, xb_words, xb_scales, offs,
         neg_mean = [tile([P, 1], F32, f"neg_mean{t}") for t in range(PACK)]
         scaled = tile([P, BANK], BF16, "scaled")
         y = tile([P, PACK, B], F32, "y")
-        y_woven = tile([P, B * PACK], BF16, "y_woven")
+        y_woven = [tile([P, B // HALVES * PACK], BF16, f"y_woven{h}") for h in range(HALVES)]
+        half = [slice(h * B // HALVES, (h + 1) * B // HALVES) for h in range(HALVES)]
         y_codes = tile([P, B], U32, "y_codes")
         y_scales = tile([P, B], U8, "y_scales")
 
@@ -69,13 +71,16 @@ def tile_list_best_of_column_groups_pl_kernel(tc, xa, xb_words, xb_scales, offs,
             rows = xa[z * P * PACK : (z + 1) * P * PACK, :].rearrange("(p t) w -> p t w", t=PACK)
             nc.sync.dma_start(out=raw[g][c][:], in_=rows[:, 2 * u : 2 * u + 2, c * (T // 2) : (c + 1) * (T // 2)])
 
+        def round_on_scalar(out, in_):
+            nc.scalar.activation(out=out, in_=in_, func=COPY)
+
+        def round_columns(g, c, start, stop, copy):
+            base = c * (T // 2)
+            copy(out=pair_table[g][:, base + start : base + stop, :], in_=raw[g][c][:, :, start:stop].rearrange("p e w -> p w e"))
+
         def round_pairs(g):
             for c in range(2):
-                nc.scalar.activation(
-                    out=pair_table[g][:, c * (T // 2) : (c + 1) * (T // 2), :],
-                    in_=raw[g][c][:].rearrange("p e w -> p w e"),
-                    func=COPY,
-                )
+                round_columns(g, c, 0, T // 2, round_on_scalar)
 
         def pick_pairs(g):
             z, u = divmod(g, 2)
@@ -85,7 +90,7 @@ def tile_list_best_of_column_groups_pl_kernel(tc, xa, xb_words, xb_scales, offs,
         def pick_words(z, h):
             cols = BANK // LIST_ROWS
             nc.vector.tensor_copy(
-                out=b_words[z][h][:], in_=word_table[z][:].indirect(list_b[:, h * cols : (h + 1) * cols])
+                out=b_words[z, h][:], in_=word_table[z][:].indirect(list_b[:, h * cols : (h + 1) * cols])
             )
 
         def weave(z, c, copy, words):
@@ -107,7 +112,7 @@ def tile_list_best_of_column_groups_pl_kernel(tc, xa, xb_words, xb_scales, offs,
                 out=acc[t][h][:],
                 lhsT=a_codes[z][:, rows].bitcast(FP8X4),
                 lhsT_scale=a_scales[z][:, rows],
-                rhs=b_words[z][h][:].bitcast(FP4X4),
+                rhs=b_words[z, h][:].bitcast(FP4X4),
                 rhs_scale=b_scales[:, z, h * BANK : (h + 1) * BANK],
                 start=(z == 0),
                 stop=(z == PASSES - 1),
@@ -137,15 +142,29 @@ def tile_list_best_of_column_groups_pl_kernel(tc, xa, xb_words, xb_scales, offs,
                     accum_out=neg_mean[t][:],
                 )
 
-        def finish_rows(t, engine):
-            engine.tensor_scalar(
-                out=y[:, t, :], in0=best[t][:], scalar1=1.0, scalar2=neg_mean[t][:], op0=MULT, op1=ADD
-            )
+        def subtract_mean(t, cols, engine):
+            if engine == "scalar":
+                nc.scalar.activation(out=y[:, t, cols], in_=best[t][:, cols], func=IDENTITY, bias=neg_mean[t][:])
+            else:
+                (nc.vector if engine == "vector" else nc.gpsimd).tensor_scalar(
+                    out=y[:, t, cols], in0=best[t][:, cols], scalar1=1.0, scalar2=neg_mean[t][:], op0=MULT, op1=ADD
+                )
+
+        def store_rows(t):
             nc.sync.dma_start(out=out_0.rearrange("(p t) b -> p t b", t=PACK)[:, t, :], in_=y[:, t, :])
 
-        nc.gpsimd.memset(scale_table[:].bitcast(I32)[32:64, :], 0)
-        nc.gpsimd.memset(scale_table[:].bitcast(I32)[64:P, :], 0)
-        nc.gpsimd.memset(b_scales[:].rearrange("p z c -> p (z c)").bitcast(I32), 0)
+        def round_y(h, copy):
+            copy(
+                out=y_woven[h][:].rearrange("p (c i t) -> p c t i", i=4, t=PACK),
+                in_=y[:, :, half[h]].rearrange("p t (c i) -> p c t i", i=4),
+            )
+
+        def quantize_y(h):
+            nc.vector.quantize_mx(out=y_codes[:, half[h]].bitcast(FP8X4), scales=y_scales[:, half[h]], in_=y_woven[h][:])
+
+        nc.vector.memset(scale_table[:].bitcast(I32)[32:64, :], 0)
+        nc.vector.memset(scale_table[:].bitcast(I32)[64:P, :], 0)
+        nc.vector.memset(b_scales[:].rearrange("p z c -> p (z c)").bitcast(I32), 0)
 
         nc.sync.dma_start(list_b[:], offs2)
         nc.sync.dma_start(
@@ -165,9 +184,9 @@ def tile_list_best_of_column_groups_pl_kernel(tc, xa, xb_words, xb_scales, offs,
                 out=b_scales[:].bitcast(I32)[32 * q : 32 * q + 4], in_=picked_scales[:].bitcast(I32)[8 * q : 8 * q + 8, :]
             )
         load_raw(2, 1)
-        load_words(1)
         load_raw(3, 0)
         load_raw(3, 1)
+        load_words(1)
         pick_words(0, 0)
         pick_words(0, 1)
         round_pairs(0)
@@ -182,36 +201,36 @@ def tile_list_best_of_column_groups_pl_kernel(tc, xa, xb_words, xb_scales, offs,
             for t in range(PACK):
                 multiply(0, t, h)
         round_pairs(2)
-        pick_words(1, 0)
         pick_pairs(2)
-        round_pairs(3)
-        pick_words(1, 1)
+        round_columns(3, 0, 0, T // 2, round_on_scalar)
+        round_columns(3, 1, 0, LAST_SPLIT, round_on_scalar)
+        round_columns(3, 1, LAST_SPLIT, T // 2, nc.vector.tensor_copy)
         pick_pairs(3)
-        weave(1, 0, nc.vector.tensor_copy, I32)
-        weave(1, 1, nc.scalar.copy, U32)
+        pick_words(1, 0)
+        for c in range(2):
+            weave(1, c, nc.scalar.copy, U32)
         for c in range(2):
             quantize_a(1, c)
-        for t0 in range(0, PACK, 2):
-            for h in range(HALVES):
-                multiply(1, t0, h)
-                multiply(1, t0 + 1, h)
-                sum_of_bank(t0, h)
-                best_of_bank(t0 + 1, h)
-                best_of_bank(t0, h)
-                sum_of_bank(t0 + 1, h)
-            for t in (t0, t0 + 1):
-                finish_rows(t, nc.gpsimd if t0 == 0 else nc.vector)
-
-        for c in range(2):
-            nc.vector.tensor_copy(
-                out=y_woven[:, c * 2 * B : (c + 1) * 2 * B].rearrange("p (c i t) -> p c t i", i=4, t=PACK),
-                in_=y[:, :, c * B // 2 : (c + 1) * B // 2].rearrange("p t (c i) -> p c t i", i=4),
-            )
-        for c in range(2):
-            cols = slice(c * B // 2, (c + 1) * B // 2)
-            nc.vector.quantize_mx(
-                out=y_codes[:, cols].bitcast(FP8X4), scales=y_scales[:, cols], in_=y_woven[:, c * 2 * B : (c + 1) * 2 * B]
-            )
+        b_words[1, 1] = tile([P, BANK], U16, "woven1_1")
+        pick_words(1, 1)
+        for h in range(HALVES):
+            for t in range(PACK):
+                multiply(1, t, h)
+                sum_of_bank(t, h)
+                best_of_bank(t, h)
+        for t in range(2):
+            subtract_mean(t, slice(0, B), "gpsimd")
+            store_rows(t)
+        subtract_mean(2, half[0], "scalar")
+        subtract_mean(3, half[0], "scalar")
+        round_y(0, nc.scalar.copy)
+        subtract_mean(2, half[1], "gpsimd")
+        store_rows(2)
+        subtract_mean(3, half[1], "vector")
+        store_rows(3)
+        quantize_y(0)
+        round_y(1, nc.vector.tensor_copy)
+        quantize_y(1)
         nc.sync.dma_start(out=out_1[0].rearrange("p c r -> p (c r)").bitcast(I32), in_=y_codes[:].bitcast(I32))
         for q in range(P // 32):
             queue = nc.scalar if q % 2 else nc.sync

@@ -130,7 +130,7 @@ def tile_list_best_of_column_groups_pl_kernel(tc, xa, xb_words, xb_scales, offs,
         def sum_of_bank(t, h):
             if h == 0:
                 nc.scalar.activation(
-                    out=scaled[:], in_=acc[t][h][:], func=IDENTITY, scale=-1.0 / (I * BANK), accum_out=carry[t][:]
+                    out=scaled[:], in_=acc[t][h][:], func=COPY, scale=-1.0 / (I * BANK), accum_out=carry[t][:]
                 )
             else:
                 nc.scalar.activation(
@@ -158,6 +158,10 @@ def tile_list_best_of_column_groups_pl_kernel(tc, xa, xb_words, xb_scales, offs,
                 out=y_woven[h][:].rearrange("p (c i t) -> p c t i", i=4, t=PACK),
                 in_=y[:, :, half[h]].rearrange("p t (c i) -> p c t i", i=4),
             )
+
+        def store_words(h):
+            words = out_1[0].rearrange("p c r -> p (c r)").bitcast(I32)
+            nc.sync.dma_start(out=words[:, half[h]], in_=y_codes[:, half[h]].bitcast(I32))
 
         def quantize_y(h):
             nc.vector.quantize_mx(out=y_codes[:, half[h]].bitcast(FP8X4), scales=y_scales[:, half[h]], in_=y_woven[h][:])
@@ -191,7 +195,9 @@ def tile_list_best_of_column_groups_pl_kernel(tc, xa, xb_words, xb_scales, offs,
         pick_words(0, 1)
         round_pairs(0)
         pick_pairs(0)
-        round_pairs(1)
+        round_columns(1, 0, 0, T // 2, round_on_scalar)
+        round_columns(1, 1, 0, LAST_SPLIT, round_on_scalar)
+        round_columns(1, 1, LAST_SPLIT, T // 2, nc.vector.tensor_copy)
         pick_pairs(1)
         for c in range(2):
             weave(0, c, nc.vector.tensor_copy, I32)
@@ -229,9 +235,10 @@ def tile_list_best_of_column_groups_pl_kernel(tc, xa, xb_words, xb_scales, offs,
         subtract_mean(3, half[1], "vector")
         store_rows(3)
         quantize_y(0)
+        store_words(0)
         round_y(1, nc.vector.tensor_copy)
         quantize_y(1)
-        nc.sync.dma_start(out=out_1[0].rearrange("p c r -> p (c r)").bitcast(I32), in_=y_codes[:].bitcast(I32))
+        store_words(1)
         for q in range(P // 32):
             queue = nc.scalar if q % 2 else nc.sync
             queue.dma_start(

@@ -151,17 +151,13 @@ def tile_list_best_of_column_groups_pl_kernel(tc, xa, xb_words, xb_scales, offs,
                 )
 
         def store_rows(t):
-            nc.sync.dma_start(out=out_0.rearrange("(p t) b -> p t b", t=PACK)[:, t, :], in_=y[:, t, :])
+            nc.sync.dma_start(out=out_0.rearrange("(p t) b -> p t b", t=PACK)[:, t : t + 2, :], in_=y[:, t : t + 2, :])
 
         def round_y(h, copy):
             copy(
                 out=y_woven[h][:].rearrange("p (c i t) -> p c t i", i=4, t=PACK),
                 in_=y[:, :, half[h]].rearrange("p t (c i) -> p c t i", i=4),
             )
-
-        def store_words(h):
-            words = out_1[0].rearrange("p c r -> p (c r)").bitcast(I32)
-            nc.sync.dma_start(out=words[:, half[h]], in_=y_codes[:, half[h]].bitcast(I32))
 
         def quantize_y(h):
             nc.vector.quantize_mx(out=y_codes[:, half[h]].bitcast(FP8X4), scales=y_scales[:, half[h]], in_=y_woven[h][:])
@@ -226,19 +222,17 @@ def tile_list_best_of_column_groups_pl_kernel(tc, xa, xb_words, xb_scales, offs,
                 best_of_bank(t, h)
         for t in range(2):
             subtract_mean(t, slice(0, B), "gpsimd")
-            store_rows(t)
+        store_rows(0)
         subtract_mean(2, half[0], "scalar")
         subtract_mean(3, half[0], "scalar")
         round_y(0, nc.scalar.copy)
         subtract_mean(2, half[1], "gpsimd")
-        store_rows(2)
         subtract_mean(3, half[1], "vector")
-        store_rows(3)
+        store_rows(2)
         quantize_y(0)
-        store_words(0)
         round_y(1, nc.vector.tensor_copy)
         quantize_y(1)
-        store_words(1)
+        nc.sync.dma_start(out=out_1[0].rearrange("p c r -> p (c r)").bitcast(I32), in_=y_codes[:].bitcast(I32))
         for q in range(P // 32):
             queue = nc.scalar if q % 2 else nc.sync
             queue.dma_start(

@@ -21,13 +21,18 @@ MAX = mybir.AluOpType.max
 AXIS_X = mybir.AxisListType.X
 
 P = 128
+QUADRANT = 32
+QUADRANTS = P // QUADRANT
 PACK = 4
 PASSES = K // (P * PACK)
+PAIRS = 2 * PASSES
+PIECE = T // 2
 BANK = 512
 HALVES = I // BANK
 GROUP = I // B
 LIST_ROWS = 16
-LAST_SPLIT = 192
+LINE = 4
+SCALAR_TOKENS = 192
 
 
 def tile_list_best_of_column_groups_pl_kernel(tc, xa, xb_words, xb_scales, offs, offs2, out_0, out_1, out_2):
@@ -43,10 +48,10 @@ def tile_list_best_of_column_groups_pl_kernel(tc, xa, xb_words, xb_scales, offs,
         list_b = tile([P, I // LIST_ROWS], U16, "list_b")
         word_table = [tile([P, S], U16, f"word_table{z}") for z in range(PASSES)]
         scale_table = tile([P, S], U8, "scale_table")
-        raw = [[tile([P, 2, T // 2], F32, f"raw{g}_{c}") for c in range(2)] for g in range(2 * PASSES)]
-        pair_table = [tile([P, T, 2], BF16, f"pair_table{g}") for g in range(2 * PASSES)]
+        raw = [[tile([P, 2, PIECE], F32, f"raw{g}_{c}") for c in range(2)] for g in range(PAIRS)]
+        pair_table = [tile([P, T, 2], BF16, f"pair_table{g}") for g in range(PAIRS)]
         picked = [tile([P, 2, J], U32, f"picked{z}") for z in range(PASSES)]
-        woven = [[tile([P, J * 2], BF16, f"woven{z}_{c}") for c in range(2)] for z in range(PASSES)]
+        woven = [[tile([P, J * 2], BF16, f"woven{z}_{d}") for d in range(2)] for z in range(PASSES)]
         a_codes = [tile([P, J], U32, f"a_codes{z}") for z in range(PASSES)]
         a_scales = [tile([P, J], U8, f"a_scales{z}") for z in range(PASSES)]
         b_words = {(z, h): tile([P, BANK], U16, f"b_words{z}_{h}") for z, h in ((0, 0), (0, 1), (1, 0))}
@@ -59,51 +64,58 @@ def tile_list_best_of_column_groups_pl_kernel(tc, xa, xb_words, xb_scales, offs,
         scaled = tile([P, BANK], BF16, "scaled")
         y = tile([P, PACK, B], F32, "y")
         y_woven = [tile([P, B // HALVES * PACK], BF16, f"y_woven{h}") for h in range(HALVES)]
-        half = [slice(h * B // HALVES, (h + 1) * B // HALVES) for h in range(HALVES)]
         y_codes = tile([P, B], U32, "y_codes")
         y_scales = tile([P, B], U8, "y_scales")
+        groups = [slice(h * B // HALVES, (h + 1) * B // HALVES) for h in range(HALVES)]
 
         def load_words(z):
             nc.sync.dma_start(out=word_table[z][:].bitcast(I32), in_=xb_words[z].bitcast(I32))
 
-        def load_raw(g, c):
+        def load_piece(g, c):
             z, u = divmod(g, 2)
-            rows = xa[z * P * PACK : (z + 1) * P * PACK, :].rearrange("(p t) w -> p t w", t=PACK)
-            nc.sync.dma_start(out=raw[g][c][:], in_=rows[:, 2 * u : 2 * u + 2, c * (T // 2) : (c + 1) * (T // 2)])
+            rows = xa[z * P * PACK : (z + 1) * P * PACK, :].rearrange("(p e) w -> p e w", e=PACK)
+            nc.sync.dma_start(out=raw[g][c][:], in_=rows[:, 2 * u : 2 * u + 2, c * PIECE : (c + 1) * PIECE])
 
-        def round_on_scalar(out, in_):
+        def scalar_cast(out, in_):
             nc.scalar.activation(out=out, in_=in_, func=COPY)
 
-        def round_columns(g, c, start, stop, copy):
-            base = c * (T // 2)
-            copy(out=pair_table[g][:, base + start : base + stop, :], in_=raw[g][c][:, :, start:stop].rearrange("p e w -> p w e"))
+        def round_tokens(g, c, start, stop, copy):
+            copy(
+                out=pair_table[g][:, c * PIECE + start : c * PIECE + stop, :],
+                in_=raw[g][c][:, :, start:stop].rearrange("p e w -> p w e"),
+            )
 
-        def round_pairs(g):
-            for c in range(2):
-                round_columns(g, c, 0, T // 2, round_on_scalar)
+        def round_pair(g):
+            round_tokens(g, 0, 0, PIECE, scalar_cast)
+            if g % 2 == 0:
+                round_tokens(g, 1, 0, PIECE, scalar_cast)
+            else:
+                round_tokens(g, 1, 0, SCALAR_TOKENS, scalar_cast)
+                round_tokens(g, 1, SCALAR_TOKENS, PIECE, nc.vector.tensor_copy)
 
-        def pick_pairs(g):
+        def pick_pair(g):
             z, u = divmod(g, 2)
             window = pair_table[g][:].rearrange("p w e -> p (w e)").bitcast(U32)
             nc.vector.tensor_copy(out=picked[z][:, u, :], in_=window.indirect(list_a[:]))
 
         def pick_words(z, h):
-            cols = BANK // LIST_ROWS
+            columns = BANK // LIST_ROWS
             nc.vector.tensor_copy(
-                out=b_words[z, h][:], in_=word_table[z][:].indirect(list_b[:, h * cols : (h + 1) * cols])
+                out=b_words[z, h][:], in_=word_table[z][:].indirect(list_b[:, h * columns : (h + 1) * columns])
             )
 
-        def weave(z, c, copy, words):
-            tiles = slice(2 * c, 2 * c + 2)
+        def weave(z, d, copy, word):
             copy(
-                out=woven[z][c][:].bitcast(words).rearrange("p (t m n u) -> p m t n u", t=2, n=2, u=2),
-                in_=picked[z][:].bitcast(words).rearrange("p u (m n t) -> p m t n u", n=2, t=PACK)[:, :, tiles],
+                out=woven[z][d][:].bitcast(word).rearrange("p (t m n u) -> p m t n u", t=2, n=2, u=2),
+                in_=picked[z][:].bitcast(word).rearrange("p u (m n t) -> p m t n u", n=2, t=PACK)[
+                    :, :, 2 * d : 2 * d + 2
+                ],
             )
 
-        def quantize_a(z, c):
-            cols = slice(c * J // 2, (c + 1) * J // 2)
+        def quantize_a(z, d):
+            columns = slice(d * J // 2, (d + 1) * J // 2)
             nc.vector.quantize_mx(
-                out=a_codes[z][:, cols].bitcast(FP8X4), scales=a_scales[z][:, cols], in_=woven[z][c][:]
+                out=a_codes[z][:, columns].bitcast(FP8X4), scales=a_scales[z][:, columns], in_=woven[z][d][:]
             )
 
         def multiply(z, t, h):
@@ -119,9 +131,8 @@ def tile_list_best_of_column_groups_pl_kernel(tc, xa, xb_words, xb_scales, offs,
             )
 
         def best_of_bank(t, h):
-            groups = BANK // GROUP
             nc.vector.tensor_reduce(
-                out=best[t][:, h * groups : (h + 1) * groups],
+                out=best[t][:, groups[h]],
                 in_=acc[t][h][:].rearrange("p (b g) -> p b g", g=GROUP),
                 axis=AXIS_X,
                 op=MAX,
@@ -142,77 +153,84 @@ def tile_list_best_of_column_groups_pl_kernel(tc, xa, xb_words, xb_scales, offs,
                     accum_out=neg_mean[t][:],
                 )
 
-        def subtract_mean(t, cols, engine):
-            if engine == "scalar":
-                nc.scalar.activation(out=y[:, t, cols], in_=best[t][:, cols], func=IDENTITY, bias=neg_mean[t][:])
-            else:
-                (nc.vector if engine == "vector" else nc.gpsimd).tensor_scalar(
-                    out=y[:, t, cols], in0=best[t][:, cols], scalar1=1.0, scalar2=neg_mean[t][:], op0=MULT, op1=ADD
-                )
+        def subtract_mean(t, h, engine):
+            engine.tensor_scalar(
+                out=y[:, t, groups[h]],
+                in0=best[t][:, groups[h]],
+                scalar1=1.0,
+                scalar2=neg_mean[t][:],
+                op0=MULT,
+                op1=ADD,
+            )
 
-        def store_rows(t):
-            nc.sync.dma_start(out=out_0.rearrange("(p t) b -> p t b", t=PACK)[:, t : t + 2, :], in_=y[:, t : t + 2, :])
+        def subtract_mean_on_scalar(t, h):
+            nc.scalar.activation(out=y[:, t, groups[h]], in_=best[t][:, groups[h]], func=IDENTITY, bias=neg_mean[t][:])
+
+        def store_two_row_tiles(t):
+            nc.sync.dma_start(
+                out=out_0.rearrange("(p t) b -> p t b", t=PACK)[:, t : t + 2, :], in_=y[:, t : t + 2, :]
+            )
 
         def round_y(h, copy):
             copy(
-                out=y_woven[h][:].rearrange("p (c i t) -> p c t i", i=4, t=PACK),
-                in_=y[:, :, half[h]].rearrange("p t (c i) -> p c t i", i=4),
+                out=y_woven[h][:].rearrange("p (c i t) -> p c t i", i=LINE, t=PACK),
+                in_=y[:, :, groups[h]].rearrange("p t (c i) -> p c t i", i=LINE),
             )
 
         def quantize_y(h):
-            nc.vector.quantize_mx(out=y_codes[:, half[h]].bitcast(FP8X4), scales=y_scales[:, half[h]], in_=y_woven[h][:])
+            nc.vector.quantize_mx(
+                out=y_codes[:, groups[h]].bitcast(FP8X4), scales=y_scales[:, groups[h]], in_=y_woven[h][:]
+            )
 
-        nc.vector.memset(scale_table[:].bitcast(I32)[32:64, :], 0)
-        nc.vector.memset(scale_table[:].bitcast(I32)[64:P, :], 0)
+        nc.vector.memset(scale_table[:].bitcast(I32)[QUADRANT : 2 * QUADRANT, :], 0)
+        nc.vector.memset(scale_table[:].bitcast(I32)[2 * QUADRANT : P, :], 0)
         nc.vector.memset(b_scales[:].rearrange("p z c -> p (z c)").bitcast(I32), 0)
 
         nc.sync.dma_start(list_b[:], offs2)
         nc.sync.dma_start(
-            out=scale_table[:].bitcast(I32)[0:32, :], in_=xb_scales.bitcast(I32).rearrange("z q c -> q z c")
+            out=scale_table[:].bitcast(I32)[0:QUADRANT, :], in_=xb_scales.bitcast(I32).rearrange("z q c -> q z c")
         )
-        load_raw(0, 0)
+        load_piece(0, 0)
         load_words(0)
         nc.sync.dma_start(list_a[:], offs)
-        load_raw(0, 1)
-        load_raw(1, 0)
-        load_raw(1, 1)
-        load_raw(2, 0)
+        load_piece(0, 1)
+        load_piece(1, 0)
+        load_piece(1, 1)
+        load_piece(2, 0)
 
         nc.vector.tensor_copy(out=picked_scales[:], in_=scale_table[:].indirect(list_b[:]))
-        for q in range(P // 32):
+        rows_moved = PACK * PASSES
+        for q in range(QUADRANTS):
             nc.sync.dma_start(
-                out=b_scales[:].bitcast(I32)[32 * q : 32 * q + 4], in_=picked_scales[:].bitcast(I32)[8 * q : 8 * q + 8, :]
+                out=b_scales[:].bitcast(I32)[QUADRANT * q : QUADRANT * q + PACK],
+                in_=picked_scales[:].bitcast(I32)[rows_moved * q : rows_moved * (q + 1), :],
             )
-        load_raw(2, 1)
-        load_raw(3, 0)
-        load_raw(3, 1)
+        load_piece(2, 1)
+        load_piece(3, 0)
+        load_piece(3, 1)
         load_words(1)
+
         pick_words(0, 0)
         pick_words(0, 1)
-        round_pairs(0)
-        pick_pairs(0)
-        round_columns(1, 0, 0, T // 2, round_on_scalar)
-        round_columns(1, 1, 0, LAST_SPLIT, round_on_scalar)
-        round_columns(1, 1, LAST_SPLIT, T // 2, nc.vector.tensor_copy)
-        pick_pairs(1)
-        for c in range(2):
-            weave(0, c, nc.vector.tensor_copy, I32)
-        for c in range(2):
-            quantize_a(0, c)
+        for g in (0, 1):
+            round_pair(g)
+            pick_pair(g)
+        for d in range(2):
+            weave(0, d, nc.vector.tensor_copy, I32)
+        for d in range(2):
+            quantize_a(0, d)
         for h in range(HALVES):
             for t in range(PACK):
                 multiply(0, t, h)
-        round_pairs(2)
-        pick_pairs(2)
-        round_columns(3, 0, 0, T // 2, round_on_scalar)
-        round_columns(3, 1, 0, LAST_SPLIT, round_on_scalar)
-        round_columns(3, 1, LAST_SPLIT, T // 2, nc.vector.tensor_copy)
-        pick_pairs(3)
+
+        for g in (2, 3):
+            round_pair(g)
+            pick_pair(g)
         pick_words(1, 0)
-        for c in range(2):
-            weave(1, c, nc.scalar.copy, U32)
-        for c in range(2):
-            quantize_a(1, c)
+        for d in range(2):
+            weave(1, d, nc.scalar.copy, U32)
+        for d in range(2):
+            quantize_a(1, d)
         b_words[1, 1] = tile([P, BANK], U16, "woven1_1")
         pick_words(1, 1)
         for h in range(HALVES):
@@ -220,21 +238,25 @@ def tile_list_best_of_column_groups_pl_kernel(tc, xa, xb_words, xb_scales, offs,
                 multiply(1, t, h)
                 sum_of_bank(t, h)
                 best_of_bank(t, h)
-        for t in range(2):
-            subtract_mean(t, slice(0, B), "gpsimd")
-        store_rows(0)
-        subtract_mean(2, half[0], "scalar")
-        subtract_mean(3, half[0], "scalar")
+
+        for t in (0, 1):
+            for h in range(HALVES):
+                subtract_mean(t, h, nc.gpsimd)
+        store_two_row_tiles(0)
+        subtract_mean(2, 0, nc.gpsimd)
+        subtract_mean_on_scalar(3, 0)
+        subtract_mean_on_scalar(2, 1)
         round_y(0, nc.scalar.copy)
-        subtract_mean(2, half[1], "gpsimd")
-        subtract_mean(3, half[1], "vector")
-        store_rows(2)
-        quantize_y(0)
+        subtract_mean(3, 1, nc.vector)
+        store_two_row_tiles(2)
         round_y(1, nc.vector.tensor_copy)
+        quantize_y(0)
         quantize_y(1)
+
         nc.sync.dma_start(out=out_1[0].rearrange("p c r -> p (c r)").bitcast(I32), in_=y_codes[:].bitcast(I32))
-        for q in range(P // 32):
+        for q in range(QUADRANTS):
             queue = nc.scalar if q % 2 else nc.sync
             queue.dma_start(
-                out=out_2[0, 4 * q : 4 * q + 4, :].bitcast(I32), in_=y_scales[:].bitcast(I32)[32 * q : 32 * q + 4, :]
+                out=out_2[0, PACK * q : PACK * (q + 1), :].bitcast(I32),
+                in_=y_scales[:].bitcast(I32)[QUADRANT * q : QUADRANT * q + PACK, :],
             )

from contextlib import ExitStack

import concourse.mybir as mybir

K, T, S, J, I, B = 1024, 1024, 2048, 512, 1024, 256
FLOPS = 2 * K * J * I

F32 = mybir.dt.float32
BF16 = mybir.dt.bfloat16
I32 = mybir.dt.int32
U32 = mybir.dt.uint32
U16 = mybir.dt.uint16
U8 = mybir.dt.uint8
FP8X4 = mybir.dt.float8_e4m3fn_x4
FP4X4 = mybir.dt.float4_e2m1fn_x4
COPY = mybir.ActivationFunctionType.Copy
IDENTITY = mybir.ActivationFunctionType.Identity
ADD = mybir.AluOpType.add
MULT = mybir.AluOpType.mult
MAX = mybir.AluOpType.max
AXIS_X = mybir.AxisListType.X

P = 128
QUADRANT = 32
QUADRANTS = P // QUADRANT
PACK = 4
PASSES = K // (P * PACK)
PAIRS = 2 * PASSES
PIECE = T // 2
BANK = 512
HALVES = I // BANK
GROUP = I // B
LIST_ROWS = 16
LINE = 4
SCALAR_TOKENS = 192


def tile_list_best_of_column_groups_pl_kernel(tc, xa, xb_words, xb_scales, offs, offs2, out_0, out_1, out_2):
    nc = tc.nc
    with ExitStack() as ctx:
        sb = ctx.enter_context(tc.tile_pool(name="sb", bufs=1))
        psum = ctx.enter_context(tc.psum_pool(name="psum", bufs=1))

        def tile(shape, dtype, name):
            return sb.tile(shape, dtype, name=name, align_bytes=64)

        list_a = tile([P, J // LIST_ROWS], U16, "list_a")
        list_b = tile([P, I // LIST_ROWS], U16, "list_b")
        word_table = [tile([P, S], U16, f"word_table{z}") for z in range(PASSES)]
        scale_table = tile([P, S], U8, "scale_table")
        raw = [[tile([P, 2, PIECE], F32, f"raw{g}_{c}") for c in range(2)] for g in range(PAIRS)]
        pair_table = [tile([P, T, 2], BF16, f"pair_table{g}") for g in range(PAIRS)]
        picked = [tile([P, 2, J], U32, f"picked{z}") for z in range(PASSES)]
        woven = [[tile([P, J * 2], BF16, f"woven{z}_{d}") for d in range(2)] for z in range(PASSES)]
        a_codes = [tile([P, J], U32, f"a_codes{z}") for z in range(PASSES)]
        a_scales = [tile([P, J], U8, f"a_scales{z}") for z in range(PASSES)]
        b_words = {(z, h): tile([P, BANK], U16, f"b_words{z}_{h}") for z, h in ((0, 0), (0, 1), (1, 0))}
        picked_scales = tile([P, I], U8, "picked_scales")
        b_scales = tile([P, PASSES, I], U8, "b_scales")
        acc = [[psum.tile([P, BANK], F32, name=f"acc{t}_{h}") for h in range(HALVES)] for t in range(PACK)]
        best = [tile([P, B], F32, f"best{t}") for t in range(PACK)]
        carry = [tile([P, 1], F32, f"carry{t}") for t in range(PACK)]
        neg_mean = [tile([P, 1], F32, f"neg_mean{t}") for t in range(PACK)]
        scaled = tile([P, BANK], BF16, "scaled")
        y = tile([P, PACK, B], F32, "y")
        y_woven = [tile([P, B // HALVES * PACK], BF16, f"y_woven{h}") for h in range(HALVES)]
        y_codes = tile([P, B], U32, "y_codes")
        y_scales = tile([P, B], U8, "y_scales")
        groups = [slice(h * B // HALVES, (h + 1) * B // HALVES) for h in range(HALVES)]

        def load_words(z):
            nc.sync.dma_start(out=word_table[z][:].bitcast(I32), in_=xb_words[z].bitcast(I32))

        def load_piece(g, c):
            z, u = divmod(g, 2)
            rows = xa[z * P * PACK : (z + 1) * P * PACK, :].rearrange("(p e) w -> p e w", e=PACK)
            nc.sync.dma_start(out=raw[g][c][:], in_=rows[:, 2 * u : 2 * u + 2, c * PIECE : (c + 1) * PIECE])

        def scalar_cast(out, in_):
            nc.scalar.activation(out=out, in_=in_, func=COPY)

        def round_tokens(g, c, start, stop, copy):
            copy(
                out=pair_table[g][:, c * PIECE + start : c * PIECE + stop, :],
                in_=raw[g][c][:, :, start:stop].rearrange("p e w -> p w e"),
            )

        def round_pair(g):
            round_tokens(g, 0, 0, PIECE, scalar_cast)
            if g % 2 == 0:
                round_tokens(g, 1, 0, PIECE, scalar_cast)
            else:
                round_tokens(g, 1, 0, SCALAR_TOKENS, scalar_cast)
                round_tokens(g, 1, SCALAR_TOKENS, PIECE, nc.vector.tensor_copy)

        def pick_pair(g):
            z, u = divmod(g, 2)
            window = pair_table[g][:].rearrange("p w e -> p (w e)").bitcast(U32)
            nc.vector.tensor_copy(out=picked[z][:, u, :], in_=window.indirect(list_a[:]))

        def pick_words(z, h):
            columns = BANK // LIST_ROWS
            nc.vector.tensor_copy(
                out=b_words[z, h][:], in_=word_table[z][:].indirect(list_b[:, h * columns : (h + 1) * columns])
            )

        def weave(z, d, copy, word):
            copy(
                out=woven[z][d][:].bitcast(word).rearrange("p (t m n u) -> p m t n u", t=2, n=2, u=2),
                in_=picked[z][:].bitcast(word).rearrange("p u (m n t) -> p m t n u", n=2, t=PACK)[
                    :, :, 2 * d : 2 * d + 2
                ],
            )

        def quantize_a(z, d):
            columns = slice(d * J // 2, (d + 1) * J // 2)
            nc.vector.quantize_mx(
                out=a_codes[z][:, columns].bitcast(FP8X4), scales=a_scales[z][:, columns], in_=woven[z][d][:]
            )

        def multiply(z, t, h):
            rows = slice(t * P, (t + 1) * P)
            nc.tensor.matmul_mx(
                out=acc[t][h][:],
                lhsT=a_codes[z][:, rows].bitcast(FP8X4),
                lhsT_scale=a_scales[z][:, rows],
                rhs=b_words[z, h][:].bitcast(FP4X4),
                rhs_scale=b_scales[:, z, h * BANK : (h + 1) * BANK],
                start=(z == 0),
                stop=(z == PASSES - 1),
            )

        def best_of_bank(t, h):
            nc.vector.tensor_reduce(
                out=best[t][:, groups[h]],
                in_=acc[t][h][:].rearrange("p (b g) -> p b g", g=GROUP),
                axis=AXIS_X,
                op=MAX,
            )

        def sum_of_bank(t, h):
            if h == 0:
                nc.scalar.activation(
                    out=scaled[:], in_=acc[t][h][:], func=COPY, scale=-1.0 / (I * BANK), accum_out=carry[t][:]
                )
            else:
                nc.scalar.activation(
                    out=scaled[:],
                    in_=acc[t][h][:],
                    func=IDENTITY,
                    scale=-1.0 / I,
                    bias=carry[t][:],
                    accum_out=neg_mean[t][:],
                )

        def subtract_mean(t, h, engine):
            engine.tensor_scalar(
                out=y[:, t, groups[h]],
                in0=best[t][:, groups[h]],
                scalar1=1.0,
                scalar2=neg_mean[t][:],
                op0=MULT,
                op1=ADD,
            )

        def subtract_mean_on_scalar(t, h):
            nc.scalar.activation(out=y[:, t, groups[h]], in_=best[t][:, groups[h]], func=IDENTITY, bias=neg_mean[t][:])

        def store_two_row_tiles(t):
            nc.sync.dma_start(
                out=out_0.rearrange("(p t) b -> p t b", t=PACK)[:, t : t + 2, :], in_=y[:, t : t + 2, :]
            )

        def round_y(h, copy):
            copy(
                out=y_woven[h][:].rearrange("p (c i t) -> p c t i", i=LINE, t=PACK),
                in_=y[:, :, groups[h]].rearrange("p t (c i) -> p c t i", i=LINE),
            )

        def quantize_y(h):
            nc.vector.quantize_mx(
                out=y_codes[:, groups[h]].bitcast(FP8X4), scales=y_scales[:, groups[h]], in_=y_woven[h][:]
            )

        nc.vector.memset(scale_table[:].bitcast(I32)[QUADRANT : 2 * QUADRANT, :], 0)
        nc.vector.memset(scale_table[:].bitcast(I32)[2 * QUADRANT : P, :], 0)
        nc.vector.memset(b_scales[:].rearrange("p z c -> p (z c)").bitcast(I32), 0)

        nc.sync.dma_start(list_b[:], offs2)
        nc.sync.dma_start(
            out=scale_table[:].bitcast(I32)[0:QUADRANT, :], in_=xb_scales.bitcast(I32).rearrange("z q c -> q z c")
        )
        load_piece(0, 0)
        load_words(0)
        nc.sync.dma_start(list_a[:], offs)
        load_piece(0, 1)
        load_piece(1, 0)
        load_piece(1, 1)
        load_piece(2, 0)

        nc.vector.tensor_copy(out=picked_scales[:], in_=scale_table[:].indirect(list_b[:]))
        rows_moved = PACK * PASSES
        for q in range(QUADRANTS):
            nc.sync.dma_start(
                out=b_scales[:].bitcast(I32)[QUADRANT * q : QUADRANT * q + PACK],
                in_=picked_scales[:].bitcast(I32)[rows_moved * q : rows_moved * (q + 1), :],
            )
        load_piece(2, 1)
        load_piece(3, 0)
        load_piece(3, 1)
        load_words(1)

        pick_words(0, 0)
        pick_words(0, 1)
        for g in (0, 1):
            round_pair(g)
            pick_pair(g)
        for d in range(2):
            weave(0, d, nc.vector.tensor_copy, I32)
        for d in range(2):
            quantize_a(0, d)
        for h in range(HALVES):
            for t in range(PACK):
                multiply(0, t, h)

        for g in (2, 3):
            round_pair(g)
            pick_pair(g)
        pick_words(1, 0)
        for d in range(2):
            weave(1, d, nc.scalar.copy, U32)
        for d in range(2):
            quantize_a(1, d)
        b_words[1, 1] = tile([P, BANK], U16, "woven1_1")
        pick_words(1, 1)
        for h in range(HALVES):
            for t in range(PACK):
                multiply(1, t, h)
                sum_of_bank(t, h)
                best_of_bank(t, h)

        for t in (0, 1):
            for h in range(HALVES):
                subtract_mean(t, h, nc.gpsimd)
        store_two_row_tiles(0)
        subtract_mean(2, 0, nc.gpsimd)
        subtract_mean_on_scalar(3, 0)
        subtract_mean_on_scalar(2, 1)
        round_y(0, nc.scalar.copy)
        subtract_mean(3, 1, nc.vector)
        store_two_row_tiles(2)
        round_y(1, nc.vector.tensor_copy)
        quantize_y(0)
        quantize_y(1)

        nc.sync.dma_start(out=out_1[0].rearrange("p c r -> p (c r)").bitcast(I32), in_=y_codes[:].bitcast(I32))
        for q in range(QUADRANTS):
            queue = nc.scalar if q % 2 else nc.sync
            queue.dma_start(
                out=out_2[0, PACK * q : PACK * (q + 1), :].bitcast(I32),
                in_=y_scales[:].bitcast(I32)[QUADRANT * q : QUADRANT * q + PACK, :],
            )
